import numpy as np
import ml_dtypes


def mxq(x, axis, fmt="e4m3"):
    dtype, down = {"e4m3": (ml_dtypes.float8_e4m3fn, 7), "e5m2": (ml_dtypes.float8_e5m2, 14)}[fmt]
    v = np.moveaxis(np.asarray(x, np.float32).astype(ml_dtypes.bfloat16).astype(np.float64), axis, -1)
    blocks = v.reshape(v.shape[:-1] + (-1, 32))
    amax = np.abs(blocks).max(-1, keepdims=True)
    byte = np.maximum(np.where(amax > 0, np.frexp(amax)[1] - 1 + 127, 0) - down, 1)
    scale = np.exp2(byte - 127.0)
    codes = (blocks / scale).astype(np.float32).astype(dtype).astype(np.float64)
    return np.moveaxis((codes * scale).reshape(v.shape), -1, axis)


WIDE = False


def mx_kscale(k):
    if not WIDE:
        return np.ones(k)
    levels = np.array([10, -10, 5, -5, 0])
    if k % 512:
        return np.exp2(np.random.permutation(np.resize(levels, k // 32))).repeat(32)
    a = np.empty((k // 512, 16))
    for p in range(k // 512):
        a[p, :8] = np.random.permutation(np.resize(levels, 8))
        for g in range(8):
            far = levels[np.abs(levels - a[p, g]) >= 10]
            a[p, g + 8] = far[np.random.randint(len(far))]
    return np.exp2(a.ravel()).repeat(32)


BF16 = ml_dtypes.bfloat16


def bf(x):
    return np.asarray(x, np.float32).astype(BF16)


def f64(x):
    return np.asarray(x).astype(np.float64)


E2M1 = np.array([0.0, 0.5, 1.0, 1.5, 2.0, 3.0, 4.0, 6.0, -0.0, -0.5, -1.0, -1.5, -2.0, -3.0, -4.0, -6.0])


def pack_weight(w, fmt):
    k, n = w.shape
    w = f64(bf(w)).reshape(k // 32, 32, n)
    amax = np.abs(w).max(1)
    if fmt == "e4m3":
        byte = np.frexp(amax)[1] - 1 + 127 - 7
    else:
        mant, ex = np.frexp(amax / 6.0)
        byte = np.where(mant > 0.5, ex, ex - 1) + 127
    byte = np.clip(np.where(amax > 0, byte, 1), 1, 254)
    scaled = (w * np.exp2(127.0 - byte)[:, None, :]).reshape(k, n).astype(np.float32)
    by_word = np.ascontiguousarray(scaled.reshape(k // 512, 128, 4, n).transpose(0, 1, 3, 2))
    if fmt == "e4m3":
        words = by_word.astype(ml_dtypes.float8_e4m3fn).view(np.uint8)
    else:
        c = by_word.astype(ml_dtypes.float4_e2m1fn).view(np.uint8) & 0xF
        words = c[..., 0::2] | (c[..., 1::2] << 4)
    return np.ascontiguousarray(words), np.ascontiguousarray(byte.astype(np.uint8).reshape(k // 512, 16, n))


def unpack_weight(words, scales, fmt):
    g, p, n, _ = words.shape
    if fmt == "e4m3":
        vals = np.ascontiguousarray(words).view(ml_dtypes.float8_e4m3fn).astype(np.float64)
    else:
        nib = np.empty((g, p, n, 4), np.uint8)
        nib[..., 0::2] = words & 0xF
        nib[..., 1::2] = words >> 4
        vals = E2M1[nib]
    vals = vals * np.repeat(np.exp2(scales.astype(np.float64) - 127.0), 8, axis=1)[..., None]
    return vals.transpose(0, 1, 3, 2).reshape(g * 512, n)
def pack4(w):
    words, scales = pack_weight(w, "e2m1")
    return words.reshape(words.shape[0], 128, -1), scales


def unpack4(words, scales):
    return unpack_weight(words.reshape(words.shape[0], 128, -1, 2), scales, "e2m1")


C, D, HI, LO = 512, 2048, 512, 2048

RIDGE = 0.5


def setup_inputs():
    s = mx_kscale(HI)
    u = mx_kscale(LO)
    t = mx_kscale(D)
    a_lo = np.random.standard_normal((LO, D)) / np.sqrt(LO) / u[:, None] * t
    z = np.random.standard_normal((D, D))
    hinv = (z + z.T) / np.sqrt(2 * D) / t[:, None]
    a_lo_words, a_lo_scales = pack4(a_lo)
    hinv_words, hinv_scales = pack4(hinv)
    return {"x": bf(np.random.standard_normal((C, D))),
            "r_hi": bf(np.random.standard_normal((HI, C)) * s[:, None]),
            "a_hi": bf(np.random.standard_normal((HI, D)) / np.sqrt(HI) / s[:, None] * t),
            "r_lo": bf(np.random.standard_normal((LO, C)) * u[:, None]),
            "a_lo_words": a_lo_words, "a_lo_scales": a_lo_scales,
            "lam": bf(RIDGE * (1 + 0.1 * np.random.standard_normal(D)) * t),
            "hinv_words": hinv_words, "hinv_scales": hinv_scales}


def reference(x, r_hi, a_hi, r_lo, a_lo_words, a_lo_scales, lam, hinv_words, hinv_scales):
    x = f64(x)
    hi = mxq(f64(r_hi), 0, "e4m3").T @ mxq(f64(a_hi), 0, "e4m3")
    lo = mxq(f64(r_lo), 0, "e4m3").T @ unpack4(a_lo_words, a_lo_scales)
    grad = hi + lo - f64(lam) * x
    step = mxq(grad, 1, "e4m3") @ unpack4(hinv_words, hinv_scales)
    return x + step

@@ -1,0 +1,342 @@
+from contextlib import ExitStack
+
+import concourse.mybir as mybir
+from concourse.masks import make_identity
+
+C, D, HI, LO = 512, 2048, 512, 2048
+FLOPS = 2 * C * D * (HI + LO) + 2 * C * D * D
+
+F32 = mybir.dt.float32
+BF16 = mybir.dt.bfloat16
+I32 = mybir.dt.int32
+U32 = mybir.dt.uint32
+U8 = mybir.dt.uint8
+FP8X4 = mybir.dt.float8_e4m3fn_x4
+FP4X4 = mybir.dt.float4_e2m1fn_x4
+ALU = mybir.AluOpType
+
+P = 128
+PACK = 4
+K_PASS = P * PACK
+N = 512
+HALF = 2 * N
+LO_PASSES = LO // K_PASS
+HI_PASS = LO_PASSES
+D_PASSES = D // K_PASS
+
+
+def tile_hessian_sketch_step_s3_kernel(tc, x, r_hi, a_hi, r_lo, a_lo_words, a_lo_scales, lam, hinv_words, hinv_scales, out):
+    nc = tc.nc
+    with ExitStack() as ctx:
+        keep = ctx.enter_context(tc.tile_pool(name="keep", bufs=1))
+        stage = ctx.enter_context(tc.tile_pool(name="stage", bufs=4))
+        psum = ctx.enter_context(tc.psum_pool(name="psum", bufs=1))
+        ctx.enter_context(tc.manual_schedule())
+
+        def kept(name, shape, dtype):
+            return keep.tile(shape, dtype, name=name, align_bytes=64)
+
+        def bank(b):
+            return psum.tile([P, N], F32, name="bank%d" % b)
+
+        ident = kept("ident", [P, P], F32)
+        lam_rows = kept("lam_rows", [P, D // P], BF16)
+        lam_all = kept("lam_all", [P, D], BF16)
+        r_raw = [kept("r_raw%d" % s, [P, PACK, C], BF16) for s in range(LO_PASSES + 1)]
+        r_codes = [kept("r_codes%d" % s, [P, C], U32) for s in range(LO_PASSES + 1)]
+        r_scales = [kept("r_scales%d" % s, [P, C], U8) for s in range(LO_PASSES + 1)]
+        hi_raw = [kept("hi_raw%d" % f, [P, PACK, N], BF16) for f in range(D // N)]
+        hi_codes = [kept("hi_codes%d" % f, [P, N], U32) for f in range(D // N)]
+        hi_scales = [kept("hi_scales%d" % f, [P, N], U8) for f in range(D // N)]
+        lo_words = [[kept("lo_words%d_%d" % (h, s), [P, 2 * HALF], U8) for s in range(LO_PASSES)] for h in range(2)]
+        lo_scales = [kept("lo_scales%d" % h, [P, LO_PASSES, HALF], U8) for h in range(2)]
+        inv_words = [kept("inv_words%d" % g, [P, 2 * D], U8) for g in range(D_PASSES)]
+        inv_scales = kept("inv_scales", [P, D_PASSES, D], U8)
+        x_sb = [[kept("x%d_%d" % (t, h), [P, HALF], BF16) for h in range(2)] for t in range(C // P)]
+        grad = [[kept("grad%d_%d" % (t, h), [P, HALF], BF16) for h in range(2)] for t in range(C // P)]
+        g_codes = [[kept("g_codes%d_%d" % (t, h), [P, 2 * P], U32) for h in range(2)] for t in range(C // P)]
+        g_scales = [[kept("g_scales%d_%d" % (t, h), [P, 2 * P], U8) for h in range(2)] for t in range(C // P)]
+
+        def load_rows(dst, rows):
+            nc.sync.dma_start(out=dst[:], in_=rows.rearrange("(p j) w -> p j w", j=PACK))
+
+        def load_r(s):
+            load_rows(r_raw[s], r_hi if s == HI_PASS else r_lo[s * K_PASS : (s + 1) * K_PASS, :])
+
+        def load_hi(f):
+            load_rows(hi_raw[f], a_hi[:, f * N : (f + 1) * N])
+
+        def load_lo(h, s):
+            nc.sync.dma_start(out=lo_words[h][s][:].bitcast(I32), in_=a_lo_words[s][:, h * 2 * HALF : (h + 1) * 2 * HALF].bitcast(I32))
+
+        def load_scales(plane, src):
+            rows = src.rearrange("g (q r) n -> r q g n", r=4)
+            for r in range(4):
+                nc.sync.dma_start(out=plane[r:P:32, :, :].bitcast(I32), in_=rows[r].bitcast(I32))
+
+        def load_x(t, h):
+            nc.sync.dma_start(out=x_sb[t][h][:], in_=x[t * P : (t + 1) * P, h * HALF : (h + 1) * HALF])
+
+        def load_inv(g):
+            nc.sync.dma_start(out=inv_words[g][:].bitcast(I32), in_=hinv_words[g].bitcast(I32))
+
+        def clear(plane):
+            nc.vector.memset(plane[:].rearrange("p g n -> p (g n)").bitcast(I32), 0)
+
+        def fresh_grouped():
+            return stage.tile([P, N, PACK], BF16, name="grouped", align_bytes=64)
+
+        def interleave(on_vector, grouped, raw, cols):
+            dst = grouped[:, cols, :].rearrange("p (c i) t -> p c t i", i=4)
+            src = raw[:, :, cols].rearrange("p t (c i) -> p c t i", i=4)
+            if on_vector:
+                nc.vector.tensor_copy(out=dst, in_=src)
+            else:
+                nc.scalar.copy(out=dst, in_=src)
+
+        def quantize(grouped, codes, scales, cols):
+            nc.vector.quantize_mx(out=codes[:, cols].bitcast(FP8X4), scales=scales[:, cols],
+                                  in_=grouped[:, cols, :].rearrange("p c t -> p (c t)"))
+
+        acc = {}
+
+        def first_pass(t, f, s, start, stop):
+            cols = slice(t * P, (t + 1) * P)
+            if s == HI_PASS:
+                rhs, rhs_scale = hi_codes[f][:].bitcast(FP8X4), hi_scales[f][:]
+            else:
+                h, k = divmod(f, 2)
+                rhs = lo_words[h][s][:, k * 2 * N : (k + 1) * 2 * N].bitcast(FP4X4)
+                rhs_scale = lo_scales[h][:, s, k * N : (k + 1) * N]
+            nc.tensor.matmul_mx(out=acc[t, f][:], lhsT=r_codes[s][:, cols].bitcast(FP8X4), lhsT_scale=r_scales[s][:, cols],
+                                rhs=rhs, rhs_scale=rhs_scale, start=start, stop=stop)
+
+        def first_group(t, f, b):
+            acc[t, f] = bank(b)
+            for s in range(LO_PASSES + 1):
+                first_pass(t, f, s, s == 0, s == HI_PASS)
+
+        ridge = {}
+
+        def ridge_term(t, f, engine):
+            ridge[t, f] = stage.tile([P, N], F32, name="ridge", bufs=8, align_bytes=64)
+            h, k = divmod(f, 2)
+            engine.tensor_tensor(out=ridge[t, f][:], in0=x_sb[t][h][:, k * N : (k + 1) * N], in1=lam_all[:, f * N : (f + 1) * N], op=ALU.mult)
+
+        def park(t, f):
+            parked = stage.tile([P, N], F32, name="parked", align_bytes=64)
+            nc.scalar.copy(out=parked[:], in_=acc[t, f][:])
+            acc[t, f] = parked
+
+        def gradient(t, f):
+            h, k = divmod(f, 2)
+            nc.vector.tensor_tensor(
+                out=grad[t][h][:, k * N : (k + 1) * N].rearrange("c (u p e) -> c u p e", u=2, e=2),
+                in0=acc[t, f][:].rearrange("c (p u e) -> c u p e", u=2, e=2),
+                in1=ridge[t, f][:].rearrange("c (p u e) -> c u p e", u=2, e=2),
+                op=ALU.subtract,
+            )
+
+        turned = {}
+
+        def turn(t, h, b):
+            turned_ps = bank(b)
+            words = grad[t][h][:].bitcast(F32)
+            for j in range(4):
+                nc.tensor.transpose(turned_ps[:, j * P : (j + 1) * P], words[:, j * P : (j + 1) * P], ident[:])
+            turned[t, h] = stage.tile([P, HALF], BF16, name="turned", align_bytes=64)
+            nc.scalar.copy(out=turned[t, h][:].bitcast(F32).rearrange("p (k c u) -> p k c u", k=2, u=2),
+                           in_=turned_ps[:].rearrange("p (k u c) -> p k c u", k=2, u=2))
+
+        def quantize_gradient(t, h):
+            nc.vector.quantize_mx(out=g_codes[t][h][:].bitcast(FP8X4), scales=g_scales[t][h][:], in_=turned[t, h][:])
+
+        step = {}
+
+        def second_group(t, f, b):
+            step[t, f] = bank(b)
+            for g in range(D_PASSES):
+                h, k = divmod(g, 2)
+                cols = slice(k * P, (k + 1) * P)
+                nc.tensor.matmul_mx(out=step[t, f][:], lhsT=g_codes[t][h][:, cols].bitcast(FP8X4), lhsT_scale=g_scales[t][h][:, cols],
+                                    rhs=inv_words[g][:, f * 2 * N : (f + 1) * 2 * N].bitcast(FP4X4),
+                                    rhs_scale=inv_scales[:, g, f * N : (f + 1) * N], start=(g == 0), stop=(g == D_PASSES - 1))
+
+        def finish(t, f):
+            h, k = divmod(f, 2)
+            result = stage.tile([P, N], F32, name="result", bufs=8, align_bytes=64)
+            nc.vector.tensor_tensor(out=result[:], in0=step[t, f][:], in1=x_sb[t][h][:, k * N : (k + 1) * N], op=ALU.add)
+            nc.sync.dma_start(out=out[t * P : (t + 1) * P, f * N : (f + 1) * N], in_=result[:])
+
+        whole = slice(0, N)
+        left, right = slice(0, N // 2), slice(N // 2, N)
+
+        clear(lo_scales[0])
+        clear(lo_scales[1])
+        clear(inv_scales)
+        make_identity(nc, ident[:])
+
+        load_r(0)
+        nc.sync.dma_start(out=lam_rows[:], in_=lam.rearrange("(p m) -> p m", p=P))
+        load_scales(lo_scales[0], a_lo_scales[:, :, 0:HALF])
+        load_lo(0, 0)
+        for s in range(1, LO_PASSES):
+            load_r(s)
+            load_lo(0, s)
+        load_r(HI_PASS)
+        load_hi(0)
+        load_hi(1)
+        load_x(0, 0)
+        load_scales(lo_scales[1], a_lo_scales[:, :, HALF:D])
+        for s in range(LO_PASSES):
+            load_lo(1, s)
+        load_x(1, 0)
+        load_hi(2)
+        load_hi(3)
+        load_x(0, 1)
+        load_x(1, 1)
+        load_x(2, 0)
+        load_scales(inv_scales, hinv_scales)
+        for g in range(D_PASSES):
+            load_inv(g)
+        load_x(2, 1)
+        load_x(3, 0)
+        load_x(3, 1)
+
+        lam_words = lam_rows[:].bitcast(F32)
+        for half in range(2):
+            spread = bank(6 + half)
+            for j in range(4):
+                column = lam_words[:, 4 * half + j : 4 * half + j + 1]
+                nc.tensor.transpose(spread[:, j * P : (j + 1) * P], column.to_broadcast([P, P]), ident[:])
+            nc.scalar.copy(out=lam_all[:].bitcast(F32).rearrange("p (n j) -> p n j", j=8)[:, :, 4 * half : 4 * half + 4],
+                           in_=spread[:].rearrange("p (j n) -> p n j", j=4))
+
+        for t in range(4):
+            for f in range(2):
+                acc[t, f] = bank(2 * t + f)
+
+        def sweep(targets, features, s):
+            for t in targets:
+                for f in features:
+                    first_pass(t, f, s, s == 0, s == HI_PASS)
+
+        def shared(raw, codes, scales):
+            grouped = fresh_grouped()
+            interleave(True, grouped, raw, left)
+            interleave(False, grouped, raw, right)
+            quantize(grouped, codes, scales, left)
+            quantize(grouped, codes, scales, right)
+
+        def on_scalar(raw):
+            grouped = fresh_grouped()
+            interleave(False, grouped, raw, whole)
+            return grouped
+
+        g0 = fresh_grouped()
+        interleave(True, g0, r_raw[0], left)
+        interleave(True, g0, r_raw[0], right)
+        quantize(g0, r_codes[0], r_scales[0], left)
+        quantize(g0, r_codes[0], r_scales[0], right)
+        sweep(range(4), range(2), 0)
+        for s in range(1, LO_PASSES):
+            shared(r_raw[s], r_codes[s], r_scales[s])
+            sweep(range(4), range(2), s)
+        shared(r_raw[HI_PASS], r_codes[HI_PASS], r_scales[HI_PASS])
+        for f in range(2):
+            shared(hi_raw[f], hi_codes[f], hi_scales[f])
+            sweep((2, 3, 0, 1) if f == 0 else (0, 2, 3, 1), [f], HI_PASS)
+
+        V = nc.vector
+        R = nc.vector
+        park(2, 0)
+        park(3, 0)
+        ridge_term(0, 0, V)
+        ridge_term(0, 1, V)
+        gradient(0, 0)
+        gradient(0, 1)
+        park(2, 1)
+        park(3, 1)
+        ridge_term(1, 0, V)
+        ridge_term(1, 1, V)
+        gradient(1, 0)
+        gradient(1, 1)
+        for t, banks in enumerate(((4, 6), (0, 1), (5, 7))):
+            for f in range(2, 4):
+                acc[t, f] = bank(banks[f - 2])
+            for s in range(LO_PASSES):
+                sweep([t], range(2, 4), s)
+        shared(hi_raw[2], hi_codes[2], hi_scales[2])
+        shared(hi_raw[3], hi_codes[3], hi_scales[3])
+        for f in range(2, 4):
+            sweep(range(3), [f], HI_PASS)
+        ridge_term(0, 2, V)
+        ridge_term(0, 3, V)
+        ridge_term(1, 2, V)
+        gradient(0, 2)
+        gradient(0, 3)
+        first_group(3, 2, 2)
+        turn(0, 0, 3)
+        turn(0, 1, 4)
+        ridge_term(1, 3, V)
+        gradient(1, 2)
+        gradient(1, 3)
+        first_group(3, 3, 6)
+        quantize_gradient(0, 0)
+        quantize_gradient(0, 1)
+        turn(1, 0, 0)
+        turn(1, 1, 1)
+        ridge_term(2, 0, V)
+        ridge_term(2, 1, V)
+        gradient(2, 0)
+        gradient(2, 1)
+        quantize_gradient(1, 0)
+        quantize_gradient(1, 1)
+        second_group(0, 0, 3)
+        second_group(0, 1, 4)
+        ridge_term(2, 2, V)
+        ridge_term(2, 3, V)
+        gradient(2, 2)
+        gradient(2, 3)
+        second_group(0, 2, 0)
+        second_group(0, 3, 1)
+        finish(0, 0)
+        finish(0, 1)
+        turn(2, 0, 5)
+        turn(2, 1, 7)
+        finish(0, 2)
+        finish(0, 3)
+        ridge_term(3, 0, R)
+        ridge_term(3, 1, R)
+        second_group(1, 0, 3)
+        second_group(1, 1, 4)
+        quantize_gradient(2, 0)
+        quantize_gradient(2, 1)
+        gradient(3, 0)
+        gradient(3, 1)
+        ridge_term(3, 2, R)
+        ridge_term(3, 3, R)
+        second_group(1, 2, 0)
+        second_group(1, 3, 1)
+        gradient(3, 2)
+        gradient(3, 3)
+        finish(1, 0)
+        finish(1, 1)
+        second_group(2, 0, 5)
+        second_group(2, 1, 7)
+        turn(3, 0, 2)
+        turn(3, 1, 6)
+        finish(1, 2)
+        finish(1, 3)
+        second_group(2, 2, 3)
+        second_group(2, 3, 4)
+        finish(2, 0)
+        finish(2, 1)
+        quantize_gradient(3, 0)
+        quantize_gradient(3, 1)
+        for f in range(4):
+            second_group(3, f, (0, 1, 5, 7)[f])
+            if f < 2:
+                finish(2, 2 + f)
+        for f in range(4):
+            finish(3, f)

@@ -23,6 +23,8 @@ HALF = 2 * N
 LO_PASSES = LO // K_PASS
 HI_PASS = LO_PASSES
 D_PASSES = D // K_PASS
+PARKED = 3
+RIDGES = 4
 
 
 def tile_hessian_sketch_step_s3_kernel(tc, x, r_hi, a_hi, r_lo, a_lo_words, a_lo_scales, lam, hinv_words, hinv_scales, out):
@@ -50,12 +52,12 @@ def tile_hessian_sketch_step_s3_kernel(tc, x, r_hi, a_hi, r_lo, a_lo_words, a_lo
         hi_scales = [kept("hi_scales%d" % f, [P, N], U8) for f in range(D // N)]
         lo_words = [[kept("lo_words%d_%d" % (h, s), [P, 2 * HALF], U8) for s in range(LO_PASSES)] for h in range(2)]
         lo_scales = [kept("lo_scales%d" % h, [P, LO_PASSES, HALF], U8) for h in range(2)]
-        inv_words = [kept("inv_words%d" % g, [P, 2 * D], U8) for g in range(D_PASSES)]
+        inv_words = [[kept("inv_words%d_%d" % (h, g), [P, 2 * HALF], U8) for g in range(D_PASSES)] for h in range(2)]
         inv_scales = kept("inv_scales", [P, D_PASSES, D], U8)
         x_sb = [[kept("x%d_%d" % (t, h), [P, HALF], BF16) for h in range(2)] for t in range(C // P)]
         grad = [[kept("grad%d_%d" % (t, h), [P, HALF], BF16) for h in range(2)] for t in range(C // P)]
-        g_codes = [[kept("g_codes%d_%d" % (t, h), [P, 2 * P], U32) for h in range(2)] for t in range(C // P)]
-        g_scales = [[kept("g_scales%d_%d" % (t, h), [P, 2 * P], U8) for h in range(2)] for t in range(C // P)]
+        g_codes = [kept("g_codes%d" % t, [P, D_PASSES * P], U32) for t in range(C // P)]
+        g_scales = [kept("g_scales%d" % t, [P, D_PASSES * P], U8) for t in range(C // P)]
 
         def load_rows(dst, rows):
             nc.sync.dma_start(out=dst[:], in_=rows.rearrange("(p j) w -> p j w", j=PACK))
@@ -77,8 +79,8 @@ def tile_hessian_sketch_step_s3_kernel(tc, x, r_hi, a_hi, r_lo, a_lo_words, a_lo
         def load_x(t, h):
             nc.sync.dma_start(out=x_sb[t][h][:], in_=x[t * P : (t + 1) * P, h * HALF : (h + 1) * HALF])
 
-        def load_inv(g):
-            nc.sync.dma_start(out=inv_words[g][:].bitcast(I32), in_=hinv_words[g].bitcast(I32))
+        def load_inv(h, g):
+            nc.sync.dma_start(out=inv_words[h][g][:].bitcast(I32), in_=hinv_words[g][:, h * 2 * HALF : (h + 1) * 2 * HALF].bitcast(I32))
 
         def clear(plane):
             nc.vector.memset(plane[:].rearrange("p g n -> p (g n)").bitcast(I32), 0)
@@ -118,55 +120,78 @@ def tile_hessian_sketch_step_s3_kernel(tc, x, r_hi, a_hi, r_lo, a_lo_words, a_lo
 
         ridge = {}
 
-        def ridge_term(t, f, engine):
-            ridge[t, f] = stage.tile([P, N], F32, name="ridge", bufs=8, align_bytes=64)
-            h, k = divmod(f, 2)
-            engine.tensor_tensor(out=ridge[t, f][:], in0=x_sb[t][h][:, k * N : (k + 1) * N], in1=lam_all[:, f * N : (f + 1) * N], op=ALU.mult)
+        def ridge_term(t, h, engine):
+            ridge[t, h] = stage.tile([P, HALF], F32, name="ridge", bufs=RIDGES, align_bytes=64)
+            if engine is nc.vector:
+                engine.tensor_tensor(out=ridge[t, h][:], in0=x_sb[t][h][:], in1=lam_all[:, h * HALF : (h + 1) * HALF], op=ALU.mult)
+            else:
+                for k in range(2):
+                    cols = slice(k * N, (k + 1) * N)
+                    engine.tensor_tensor(out=ridge[t, h][:, cols], in0=x_sb[t][h][:, cols], in1=lam_all[:, h * HALF + k * N : h * HALF + (k + 1) * N], op=ALU.mult)
+
+        parked = {}
 
         def park(t, f):
-            parked = stage.tile([P, N], F32, name="parked", align_bytes=64)
-            nc.scalar.copy(out=parked[:], in_=acc[t, f][:])
-            acc[t, f] = parked
+            h, k = divmod(f, 2)
+            if (t, h) not in parked:
+                parked[t, h] = stage.tile([P, HALF], F32, name="parked", bufs=PARKED, align_bytes=64)
+            nc.scalar.copy(out=parked[t, h][:, k * N : (k + 1) * N], in_=acc[t, f][:])
 
         def gradient(t, f):
             h, k = divmod(f, 2)
+            cols = slice(k * N, (k + 1) * N)
             nc.vector.tensor_tensor(
-                out=grad[t][h][:, k * N : (k + 1) * N].rearrange("c (u p e) -> c u p e", u=2, e=2),
+                out=grad[t][h][:, cols].rearrange("c (u p e) -> c u p e", u=2, e=2),
                 in0=acc[t, f][:].rearrange("c (p u e) -> c u p e", u=2, e=2),
-                in1=ridge[t, f][:].rearrange("c (p u e) -> c u p e", u=2, e=2),
+                in1=ridge[t, h][:, cols].rearrange("c (p u e) -> c u p e", u=2, e=2),
+                op=ALU.subtract,
+            )
+
+        def parked_gradient(t, h):
+            nc.vector.tensor_tensor(
+                out=grad[t][h][:].rearrange("c (u q e) -> c u q e", u=2, e=2),
+                in0=parked[t, h][:].rearrange("c (q u e) -> c u q e", u=2, e=2),
+                in1=ridge[t, h][:].rearrange("c (q u e) -> c u q e", u=2, e=2),
                 op=ALU.subtract,
             )
 
         turned = {}
 
-        def turn(t, h, b):
-            turned_ps = bank(b)
-            words = grad[t][h][:].bitcast(F32)
-            for j in range(4):
-                nc.tensor.transpose(turned_ps[:, j * P : (j + 1) * P], words[:, j * P : (j + 1) * P], ident[:])
-            turned[t, h] = stage.tile([P, HALF], BF16, name="turned", align_bytes=64)
-            nc.scalar.copy(out=turned[t, h][:].bitcast(F32).rearrange("p (k c u) -> p k c u", k=2, u=2),
-                           in_=turned_ps[:].rearrange("p (k u c) -> p k c u", k=2, u=2))
+        def turn(t, banks):
+            turned[t] = stage.tile([P, D], BF16, name="turned", bufs=2, align_bytes=64)
+            turned_ps = [bank(b) for b in banks]
+            for h in range(2):
+                words = grad[t][h][:].bitcast(F32)
+                for j in range(4):
+                    nc.tensor.transpose(turned_ps[h][:, j * P : (j + 1) * P], words[:, j * P : (j + 1) * P], ident[:])
+                nc.scalar.copy(out=turned[t][:, h * HALF : (h + 1) * HALF].bitcast(F32).rearrange("p (k c u) -> p k c u", k=2, u=2),
+                               in_=turned_ps[h][:].rearrange("p (u k c) -> p k c u" if (t, h) in parked else "p (k u c) -> p k c u", k=2, u=2))
 
-        def quantize_gradient(t, h):
-            nc.vector.quantize_mx(out=g_codes[t][h][:].bitcast(FP8X4), scales=g_scales[t][h][:], in_=turned[t, h][:])
+        def quantize_gradient(t):
+            nc.vector.quantize_mx(out=g_codes[t][:].bitcast(FP8X4), scales=g_scales[t][:], in_=turned[t][:])
 
         step = {}
 
+        def second_passes(dst, t, first, width):
+            h, offset = divmod(first, HALF)
+            for g in range(D_PASSES):
+                cols = slice(g * P, (g + 1) * P)
+                nc.tensor.matmul_mx(out=dst, lhsT=g_codes[t][:, cols].bitcast(FP8X4), lhsT_scale=g_scales[t][:, cols],
+                                    rhs=inv_words[h][g][:, 2 * offset : 2 * (offset + width)].bitcast(FP4X4),
+                                    rhs_scale=inv_scales[:, g, first : first + width], start=(g == 0), stop=(g == D_PASSES - 1))
+
         def second_group(t, f, b):
             step[t, f] = bank(b)
-            for g in range(D_PASSES):
-                h, k = divmod(g, 2)
-                cols = slice(k * P, (k + 1) * P)
-                nc.tensor.matmul_mx(out=step[t, f][:], lhsT=g_codes[t][h][:, cols].bitcast(FP8X4), lhsT_scale=g_scales[t][h][:, cols],
-                                    rhs=inv_words[g][:, f * 2 * N : (f + 1) * 2 * N].bitcast(FP4X4),
-                                    rhs_scale=inv_scales[:, g, f * N : (f + 1) * N], start=(g == 0), stop=(g == D_PASSES - 1))
+            second_passes(step[t, f][:], t, f * N, N)
+
+        def add_and_store(src, t, first, width):
+            h, offset = divmod(first, HALF)
+            result = stage.tile([P, width], F32, name="result", bufs=8, align_bytes=64)
+            nc.vector.tensor_tensor(out=result[:], in0=src, in1=x_sb[t][h][:, offset : offset + width], op=ALU.add)
+            nc.sync.dma_start(out=out[t * P : (t + 1) * P, first : first + width], in_=result[:])
 
         def finish(t, f):
-            h, k = divmod(f, 2)
-            result = stage.tile([P, N], F32, name="result", bufs=8, align_bytes=64)
-            nc.vector.tensor_tensor(out=result[:], in0=step[t, f][:], in1=x_sb[t][h][:, k * N : (k + 1) * N], op=ALU.add)
-            nc.sync.dma_start(out=out[t * P : (t + 1) * P, f * N : (f + 1) * N], in_=result[:])
+            add_and_store(step[t, f][:], t, f * N, N)
 
         whole = slice(0, N)
         left, right = slice(0, N // 2), slice(N // 2, N)
@@ -188,33 +213,24 @@ def tile_hessian_sketch_step_s3_kernel(tc, x, r_hi, a_hi, r_lo, a_lo_words, a_lo
         load_hi(1)
         load_x(0, 0)
         load_scales(lo_scales[1], a_lo_scales[:, :, HALF:D])
-        for s in range(LO_PASSES):
-            load_lo(1, s)
+        load_lo(1, 0)
         load_x(1, 0)
+        for s in range(1, LO_PASSES):
+            load_lo(1, s)
         load_hi(2)
         load_hi(3)
         load_x(0, 1)
         load_x(1, 1)
-        load_x(2, 0)
         load_scales(inv_scales, hinv_scales)
+        load_x(2, 0)
         for g in range(D_PASSES):
-            load_inv(g)
+            load_inv(0, g)
         load_x(2, 1)
+        for g in range(D_PASSES):
+            load_inv(1, g)
         load_x(3, 0)
         load_x(3, 1)
 
-        lam_words = lam_rows[:].bitcast(F32)
-        for half in range(2):
-            spread = bank(6 + half)
-            for j in range(4):
-                column = lam_words[:, 4 * half + j : 4 * half + j + 1]
-                nc.tensor.transpose(spread[:, j * P : (j + 1) * P], column.to_broadcast([P, P]), ident[:])
-            nc.scalar.copy(out=lam_all[:].bitcast(F32).rearrange("p (n j) -> p n j", j=8)[:, :, 4 * half : 4 * half + 4],
-                           in_=spread[:].rearrange("p (j n) -> p n j", j=4))
-
-        for t in range(4):
-            for f in range(2):
-                acc[t, f] = bank(2 * t + f)
 
         def sweep(targets, features, s):
             for t in targets:
@@ -225,8 +241,7 @@ def tile_hessian_sketch_step_s3_kernel(tc, x, r_hi, a_hi, r_lo, a_lo_words, a_lo
             grouped = fresh_grouped()
             interleave(True, grouped, raw, left)
             interleave(False, grouped, raw, right)
-            quantize(grouped, codes, scales, left)
-            quantize(grouped, codes, scales, right)
+            quantize(grouped, codes, scales, whole)
 
         def on_scalar(raw):
             grouped = fresh_grouped()
@@ -235,9 +250,20 @@ def tile_hessian_sketch_step_s3_kernel(tc, x, r_hi, a_hi, r_lo, a_lo_words, a_lo
 
         g0 = fresh_grouped()
         interleave(True, g0, r_raw[0], left)
-        interleave(True, g0, r_raw[0], right)
+        interleave(False, g0, r_raw[0], right)
         quantize(g0, r_codes[0], r_scales[0], left)
         quantize(g0, r_codes[0], r_scales[0], right)
+        lam_words = lam_rows[:].bitcast(F32)
+        for half in range(2):
+            spread = bank(6 + half)
+            for j in range(4):
+                column = lam_words[:, 4 * half + j : 4 * half + j + 1]
+                nc.tensor.transpose(spread[:, j * P : (j + 1) * P], column.to_broadcast([P, P]), ident[:])
+            nc.scalar.copy(out=lam_all[:].bitcast(F32).rearrange("p (n j) -> p n j", j=8)[:, :, 4 * half : 4 * half + 4],
+                           in_=spread[:].rearrange("p (j n) -> p n j", j=4))
+        for t in range(4):
+            for f in range(2):
+                acc[t, f] = bank(2 * t + f)
         sweep(range(4), range(2), 0)
         for s in range(1, LO_PASSES):
             shared(r_raw[s], r_codes[s], r_scales[s])
@@ -248,95 +274,95 @@ def tile_hessian_sketch_step_s3_kernel(tc, x, r_hi, a_hi, r_lo, a_lo_words, a_lo
             sweep((2, 3, 0, 1) if f == 0 else (0, 2, 3, 1), [f], HI_PASS)
 
         V = nc.vector
-        R = nc.vector
+        R = nc.gpsimd
         park(2, 0)
         park(3, 0)
         ridge_term(0, 0, V)
-        ridge_term(0, 1, V)
-        gradient(0, 0)
-        gradient(0, 1)
         park(2, 1)
         park(3, 1)
+        park(1, 0)
+        park(1, 1)
         ridge_term(1, 0, V)
-        ridge_term(1, 1, V)
-        gradient(1, 0)
-        gradient(1, 1)
-        for t, banks in enumerate(((4, 6), (0, 1), (5, 7))):
+        gradient(0, 0)
+        gradient(0, 1)
+        parked_gradient(1, 0)
+        for t, banks in enumerate(((4, 6), (5, 7), (2, 3))):
             for f in range(2, 4):
                 acc[t, f] = bank(banks[f - 2])
             for s in range(LO_PASSES):
                 sweep([t], range(2, 4), s)
         shared(hi_raw[2], hi_codes[2], hi_scales[2])
-        shared(hi_raw[3], hi_codes[3], hi_scales[3])
+        g3 = fresh_grouped()
+        interleave(True, g3, hi_raw[3], left)
+        interleave(False, g3, hi_raw[3], right)
+        ridge_term(0, 1, V)
+        quantize(g3, hi_codes[3], hi_scales[3], whole)
         for f in range(2, 4):
             sweep(range(3), [f], HI_PASS)
-        ridge_term(0, 2, V)
-        ridge_term(0, 3, V)
-        ridge_term(1, 2, V)
+        ridge_term(1, 1, V)
+        ridge_term(2, 0, R)
         gradient(0, 2)
         gradient(0, 3)
-        first_group(3, 2, 2)
-        turn(0, 0, 3)
-        turn(0, 1, 4)
-        ridge_term(1, 3, V)
+        acc[3, 2] = bank(0)
+        for s in range(2):
+            first_pass(3, 2, s, s == 0, False)
+        turn(0, (1, 4))
+        for s in range(2, LO_PASSES + 1):
+            first_pass(3, 2, s, False, s == HI_PASS)
         gradient(1, 2)
         gradient(1, 3)
+        ridge_term(2, 1, R)
         first_group(3, 3, 6)
-        quantize_gradient(0, 0)
-        quantize_gradient(0, 1)
-        turn(1, 0, 0)
-        turn(1, 1, 1)
-        ridge_term(2, 0, V)
-        ridge_term(2, 1, V)
-        gradient(2, 0)
-        gradient(2, 1)
-        quantize_gradient(1, 0)
-        quantize_gradient(1, 1)
-        second_group(0, 0, 3)
-        second_group(0, 1, 4)
-        ridge_term(2, 2, V)
-        ridge_term(2, 3, V)
+        quantize_gradient(0)
+        second_group(0, 0, 5)
+        turn(1, (7, 1))
+        parked_gradient(2, 0)
         gradient(2, 2)
         gradient(2, 3)
-        second_group(0, 2, 0)
-        second_group(0, 3, 1)
-        finish(0, 0)
-        finish(0, 1)
-        turn(2, 0, 5)
-        turn(2, 1, 7)
-        finish(0, 2)
-        finish(0, 3)
         ridge_term(3, 0, R)
         ridge_term(3, 1, R)
-        second_group(1, 0, 3)
+        second_group(0, 1, 4)
+        quantize_gradient(1)
+        finish(0, 0)
+        second_group(0, 2, 2)
+        second_group(0, 3, 3)
+        finish(0, 1)
+        turn(2, (7, 1))
+        finish(0, 2)
+        finish(0, 3)
+        second_group(1, 0, 5)
         second_group(1, 1, 4)
-        quantize_gradient(2, 0)
-        quantize_gradient(2, 1)
-        gradient(3, 0)
-        gradient(3, 1)
-        ridge_term(3, 2, R)
-        ridge_term(3, 3, R)
-        second_group(1, 2, 0)
-        second_group(1, 3, 1)
+        finish(1, 0)
+        quantize_gradient(2)
+        parked_gradient(3, 0)
         gradient(3, 2)
         gradient(3, 3)
-        finish(1, 0)
+        second_group(1, 2, 2)
+        second_group(1, 3, 3)
         finish(1, 1)
         second_group(2, 0, 5)
-        second_group(2, 1, 7)
-        turn(3, 0, 2)
-        turn(3, 1, 6)
+        second_group(2, 1, 0)
+        turn(3, (7, 1))
         finish(1, 2)
         finish(1, 3)
-        second_group(2, 2, 3)
-        second_group(2, 3, 4)
+        second_group(2, 2, 6)
         finish(2, 0)
+        quantize_gradient(3)
+        second_group(2, 3, 4)
         finish(2, 1)
-        quantize_gradient(3, 0)
-        quantize_gradient(3, 1)
-        for f in range(4):
-            second_group(3, f, (0, 1, 5, 7)[f])
-            if f < 2:
-                finish(2, 2 + f)
-        for f in range(4):
-            finish(3, f)
+        finish(2, 2)
+        second_group(3, 0, 2)
+        second_group(3, 1, 3)
+        second_group(3, 2, 5)
+        finish(2, 3)
+        finish(3, 0)
+        finish(3, 1)
+        pieces = []
+        for b, first, width in ((0, 3 * N, 2 * P), (7, 3 * N + 2 * P, P), (1, 3 * N + 3 * P, P)):
+            piece = bank(b)
+            for q in range(0, width, P):
+                second_passes(piece[:, q : q + P], 3, first + q, P)
+            pieces.append((piece[:, 0:width], 3, first, width))
+        finish(3, 2)
+        for piece in pieces:
+            add_and_store(*piece)

@@ -89,8 +89,8 @@ def tile_hessian_sketch_step_s3_kernel(tc, x, r_hi, a_hi, r_lo, a_lo_words, a_lo
             return stage.tile([P, N, PACK], BF16, name="grouped", align_bytes=64)
 
         def interleave(on_vector, grouped, raw, cols):
-            dst = grouped[:, cols, :].rearrange("p (c i) t -> p c t i", i=4)
-            src = raw[:, :, cols].rearrange("p t (c i) -> p c t i", i=4)
+            dst = grouped[:, cols, :]
+            src = raw[:, :, cols].rearrange("p t c -> p c t")
             if on_vector:
                 nc.vector.tensor_copy(out=dst, in_=src)
             else:

@@ -18,16 +18,21 @@ ALU = mybir.AluOpType
 P = 128
 PACK = 4
 K_PASS = P * PACK
-N = 512
-HALF = 2 * N
+CHUNK = 512
+HALF = 2 * CHUNK
+TILES = C // P
+CHUNKS = D // CHUNK
 LO_PASSES = LO // K_PASS
 HI_PASS = LO_PASSES
 D_PASSES = D // K_PASS
-PARKED = 3
-RIDGES = 4
+BANKS = 8
+FP4_BYTES = 2
+AHEAD_OF_TURN = 2
 
 
-def tile_hessian_sketch_step_s3_kernel(tc, x, r_hi, a_hi, r_lo, a_lo_words, a_lo_scales, lam, hinv_words, hinv_scales, out):
+def tile_hessian_sketch_step_s3_kernel(
+    tc, x, r_hi, a_hi, r_lo, a_lo_words, a_lo_scales, lam, hinv_words, hinv_scales, out
+):
     nc = tc.nc
     with ExitStack() as ctx:
         keep = ctx.enter_context(tc.tile_pool(name="keep", bufs=1))
@@ -38,116 +43,126 @@ def tile_hessian_sketch_step_s3_kernel(tc, x, r_hi, a_hi, r_lo, a_lo_words, a_lo
         def kept(name, shape, dtype):
             return keep.tile(shape, dtype, name=name, align_bytes=64)
 
-        def bank(b):
-            return psum.tile([P, N], F32, name="bank%d" % b)
-
         ident = kept("ident", [P, P], F32)
         lam_rows = kept("lam_rows", [P, D // P], BF16)
         lam_all = kept("lam_all", [P, D], BF16)
         r_raw = [kept("r_raw%d" % s, [P, PACK, C], BF16) for s in range(LO_PASSES + 1)]
         r_codes = [kept("r_codes%d" % s, [P, C], U32) for s in range(LO_PASSES + 1)]
         r_scales = [kept("r_scales%d" % s, [P, C], U8) for s in range(LO_PASSES + 1)]
-        hi_raw = [kept("hi_raw%d" % f, [P, PACK, N], BF16) for f in range(D // N)]
-        hi_codes = [kept("hi_codes%d" % f, [P, N], U32) for f in range(D // N)]
-        hi_scales = [kept("hi_scales%d" % f, [P, N], U8) for f in range(D // N)]
-        lo_words = [[kept("lo_words%d_%d" % (h, s), [P, 2 * HALF], U8) for s in range(LO_PASSES)] for h in range(2)]
+        hi_raw = [kept("hi_raw%d" % f, [P, PACK, CHUNK], BF16) for f in range(CHUNKS)]
+        hi_codes = [kept("hi_codes%d" % f, [P, CHUNK], U32) for f in range(CHUNKS)]
+        hi_scales = [kept("hi_scales%d" % f, [P, CHUNK], U8) for f in range(CHUNKS)]
+        lo_words = [[kept("lo_words%d_%d" % (h, s), [P, FP4_BYTES * HALF], U8) for s in range(LO_PASSES)] for h in range(2)]
         lo_scales = [kept("lo_scales%d" % h, [P, LO_PASSES, HALF], U8) for h in range(2)]
-        inv_words = [[kept("inv_words%d_%d" % (h, g), [P, 2 * HALF], U8) for g in range(D_PASSES)] for h in range(2)]
-        inv_scales = kept("inv_scales", [P, D_PASSES, D], U8)
-        x_sb = [[kept("x%d_%d" % (t, h), [P, HALF], BF16) for h in range(2)] for t in range(C // P)]
-        grad = [[kept("grad%d_%d" % (t, h), [P, HALF], BF16) for h in range(2)] for t in range(C // P)]
-        g_codes = [kept("g_codes%d" % t, [P, D_PASSES * P], U32) for t in range(C // P)]
-        g_scales = [kept("g_scales%d" % t, [P, D_PASSES * P], U8) for t in range(C // P)]
+        inv_words = [[kept("inv_words%d_%d" % (h, g), [P, FP4_BYTES * HALF], U8) for g in range(D_PASSES)] for h in range(2)]
+        inv_scales = [kept("inv_scales%d" % h, [P, D_PASSES, HALF], U8) for h in range(2)]
+        x_sb = [[kept("x%d_%d" % (t, h), [P, HALF], BF16) for h in range(2)] for t in range(TILES)]
+        grad = [[kept("grad%d_%d" % (t, h), [P, HALF], BF16) for h in range(2)] for t in range(TILES)]
+        g_codes = [kept("g_codes%d" % t, [P, D_PASSES * P], U32) for t in range(TILES)]
+        g_scales = [kept("g_scales%d" % t, [P, D_PASSES * P], U8) for t in range(TILES)]
+
+        free_banks = list(range(BANKS))
+        held = {}
+
+        def take_bank(key):
+            b = free_banks[0]
+            free_banks.remove(b)
+            held[key] = (b, psum.tile([P, CHUNK], F32, name="bank%d" % b))
+            return held[key][1]
+
+        def give_back(key):
+            free_banks.append(held[key][0])
+
+        def half_of(h, bytes_a_column=1):
+            return slice(h * HALF * bytes_a_column, (h + 1) * HALF * bytes_a_column)
 
         def load_rows(dst, rows):
-            nc.sync.dma_start(out=dst[:], in_=rows.rearrange("(p j) w -> p j w", j=PACK))
+            nc.sync.dma_start(out=dst[:], in_=rows.rearrange("(p t) w -> p t w", t=PACK))
 
         def load_r(s):
             load_rows(r_raw[s], r_hi if s == HI_PASS else r_lo[s * K_PASS : (s + 1) * K_PASS, :])
 
         def load_hi(f):
-            load_rows(hi_raw[f], a_hi[:, f * N : (f + 1) * N])
+            load_rows(hi_raw[f], a_hi[:, f * CHUNK : (f + 1) * CHUNK])
 
-        def load_lo(h, s):
-            nc.sync.dma_start(out=lo_words[h][s][:].bitcast(I32), in_=a_lo_words[s][:, h * 2 * HALF : (h + 1) * 2 * HALF].bitcast(I32))
+        def load_words(dst, words, h):
+            nc.sync.dma_start(out=dst[:].bitcast(I32), in_=words[:, half_of(h, FP4_BYTES)].bitcast(I32))
 
-        def load_scales(plane, src):
-            rows = src.rearrange("g (q r) n -> r q g n", r=4)
+        def load_scales(dst, scales, h):
+            rows = scales[:, :, half_of(h)].rearrange("g (q r) n -> r q g n", r=4)
             for r in range(4):
-                nc.sync.dma_start(out=plane[r:P:32, :, :].bitcast(I32), in_=rows[r].bitcast(I32))
+                nc.sync.dma_start(out=dst[r:P:32, :, :].bitcast(I32), in_=rows[r].bitcast(I32))
 
         def load_x(t, h):
-            nc.sync.dma_start(out=x_sb[t][h][:], in_=x[t * P : (t + 1) * P, h * HALF : (h + 1) * HALF])
+            nc.sync.dma_start(out=x_sb[t][h][:], in_=x[t * P : (t + 1) * P, half_of(h)])
 
-        def load_inv(h, g):
-            nc.sync.dma_start(out=inv_words[h][g][:].bitcast(I32), in_=hinv_words[g][:, h * 2 * HALF : (h + 1) * 2 * HALF].bitcast(I32))
+        whole = slice(0, CHUNK)
+        left, right = slice(0, CHUNK // 2), slice(CHUNK // 2, CHUNK)
 
-        def clear(plane):
-            nc.vector.memset(plane[:].rearrange("p g n -> p (g n)").bitcast(I32), 0)
+        def interleave(raw, on_vector=left, on_scalar=right):
+            grouped = stage.tile([P, CHUNK, PACK], BF16, name="grouped", align_bytes=64)
+            dst, src = "p (c i) t -> p c t i", "p t (c i) -> p c t i"
+            nc.vector.tensor_copy(out=grouped[:, on_vector, :].rearrange(dst, i=4), in_=raw[:, :, on_vector].rearrange(src, i=4))
+            nc.scalar.copy(out=grouped[:, on_scalar, :].rearrange(dst, i=4), in_=raw[:, :, on_scalar].rearrange(src, i=4))
+            return grouped
 
-        def fresh_grouped():
-            return stage.tile([P, N, PACK], BF16, name="grouped", align_bytes=64)
+        def quantize(grouped, codes, scales, cols=whole):
+            nc.vector.quantize_mx(
+                out=codes[:, cols].bitcast(FP8X4),
+                scales=scales[:, cols],
+                in_=grouped[:, cols, :].rearrange("p c t -> p (c t)"),
+            )
 
-        def interleave(on_vector, grouped, raw, cols):
-            dst = grouped[:, cols, :]
-            src = raw[:, :, cols].rearrange("p t c -> p c t")
-            if on_vector:
-                nc.vector.tensor_copy(out=dst, in_=src)
-            else:
-                nc.scalar.copy(out=dst, in_=src)
-
-        def quantize(grouped, codes, scales, cols):
-            nc.vector.quantize_mx(out=codes[:, cols].bitcast(FP8X4), scales=scales[:, cols],
-                                  in_=grouped[:, cols, :].rearrange("p c t -> p (c t)"))
-
-        acc = {}
-
-        def first_pass(t, f, s, start, stop):
+        def first_pass(t, f, s):
+            acc = take_bank(("sums", t, f)) if s == 0 else held["sums", t, f][1]
             cols = slice(t * P, (t + 1) * P)
             if s == HI_PASS:
                 rhs, rhs_scale = hi_codes[f][:].bitcast(FP8X4), hi_scales[f][:]
             else:
-                h, k = divmod(f, 2)
-                rhs = lo_words[h][s][:, k * 2 * N : (k + 1) * 2 * N].bitcast(FP4X4)
-                rhs_scale = lo_scales[h][:, s, k * N : (k + 1) * N]
-            nc.tensor.matmul_mx(out=acc[t, f][:], lhsT=r_codes[s][:, cols].bitcast(FP8X4), lhsT_scale=r_scales[s][:, cols],
-                                rhs=rhs, rhs_scale=rhs_scale, start=start, stop=stop)
+                h, j = divmod(f, 2)
+                rhs = lo_words[h][s][:, j * FP4_BYTES * CHUNK : (j + 1) * FP4_BYTES * CHUNK].bitcast(FP4X4)
+                rhs_scale = lo_scales[h][:, s, j * CHUNK : (j + 1) * CHUNK]
+            nc.tensor.matmul_mx(
+                out=acc[:],
+                lhsT=r_codes[s][:, cols].bitcast(FP8X4),
+                lhsT_scale=r_scales[s][:, cols],
+                rhs=rhs,
+                rhs_scale=rhs_scale,
+                start=(s == 0),
+                stop=(s == HI_PASS),
+            )
 
-        def first_group(t, f, b):
-            acc[t, f] = bank(b)
-            for s in range(LO_PASSES + 1):
-                first_pass(t, f, s, s == 0, s == HI_PASS)
+        def first_passes(tiles, chunks, passes):
+            for s in passes:
+                for t in tiles:
+                    for f in chunks:
+                        first_pass(t, f, s)
 
-        ridge = {}
+        ridge, parked, turned = {}, {}, {}
 
-        def ridge_term(t, h, engine):
-            ridge[t, h] = stage.tile([P, HALF], F32, name="ridge", bufs=RIDGES, align_bytes=64)
-            if engine is nc.vector:
-                engine.tensor_tensor(out=ridge[t, h][:], in0=x_sb[t][h][:], in1=lam_all[:, h * HALF : (h + 1) * HALF], op=ALU.mult)
-            else:
-                for k in range(2):
-                    cols = slice(k * N, (k + 1) * N)
-                    engine.tensor_tensor(out=ridge[t, h][:, cols], in0=x_sb[t][h][:, cols], in1=lam_all[:, h * HALF + k * N : h * HALF + (k + 1) * N], op=ALU.mult)
-
-        parked = {}
+        def ridge_term(t, h):
+            ridge[t, h] = stage.tile([P, HALF], F32, name="ridge", bufs=3, align_bytes=64)
+            nc.vector.tensor_tensor(out=ridge[t, h][:], in0=x_sb[t][h][:], in1=lam_all[:, half_of(h)], op=ALU.mult)
 
         def park(t, f):
-            h, k = divmod(f, 2)
+            h, j = divmod(f, 2)
             if (t, h) not in parked:
-                parked[t, h] = stage.tile([P, HALF], F32, name="parked", bufs=PARKED, align_bytes=64)
-            nc.scalar.copy(out=parked[t, h][:, k * N : (k + 1) * N], in_=acc[t, f][:])
+                parked[t, h] = stage.tile([P, HALF], F32, name="parked", bufs=5, align_bytes=64)
+            nc.scalar.copy(out=parked[t, h][:, j * CHUNK : (j + 1) * CHUNK], in_=held["sums", t, f][1][:])
+            give_back(("sums", t, f))
 
-        def gradient(t, f):
-            h, k = divmod(f, 2)
-            cols = slice(k * N, (k + 1) * N)
+        def gradient_from_bank(t, f):
+            h, j = divmod(f, 2)
+            cols = slice(j * CHUNK, (j + 1) * CHUNK)
             nc.vector.tensor_tensor(
                 out=grad[t][h][:, cols].rearrange("c (u p e) -> c u p e", u=2, e=2),
-                in0=acc[t, f][:].rearrange("c (p u e) -> c u p e", u=2, e=2),
+                in0=held["sums", t, f][1][:].rearrange("c (p u e) -> c u p e", u=2, e=2),
                 in1=ridge[t, h][:, cols].rearrange("c (p u e) -> c u p e", u=2, e=2),
                 op=ALU.subtract,
             )
+            give_back(("sums", t, f))
 
-        def parked_gradient(t, h):
+        def gradient_from_parked(t, h):
             nc.vector.tensor_tensor(
                 out=grad[t][h][:].rearrange("c (u q e) -> c u q e", u=2, e=2),
                 in0=parked[t, h][:].rearrange("c (q u e) -> c u q e", u=2, e=2),
@@ -155,214 +170,182 @@ def tile_hessian_sketch_step_s3_kernel(tc, x, r_hi, a_hi, r_lo, a_lo_words, a_lo
                 op=ALU.subtract,
             )
 
-        turned = {}
-
-        def turn(t, banks):
+        def turn(t):
             turned[t] = stage.tile([P, D], BF16, name="turned", bufs=2, align_bytes=64)
-            turned_ps = [bank(b) for b in banks]
+            banks = [take_bank(("turned", t, h)) for h in range(2)]
             for h in range(2):
                 words = grad[t][h][:].bitcast(F32)
-                for j in range(4):
-                    nc.tensor.transpose(turned_ps[h][:, j * P : (j + 1) * P], words[:, j * P : (j + 1) * P], ident[:])
-                nc.scalar.copy(out=turned[t][:, h * HALF : (h + 1) * HALF].bitcast(F32).rearrange("p (k c u) -> p k c u", k=2, u=2),
-                               in_=turned_ps[h][:].rearrange("p (u k c) -> p k c u" if (t, h) in parked else "p (k u c) -> p k c u", k=2, u=2))
+                for run in range(4):
+                    nc.tensor.transpose(banks[h][:, run * P : (run + 1) * P], words[:, run * P : (run + 1) * P], ident[:])
+                runs = "p (u j c) -> p j c u" if (t, h) in parked else "p (j u c) -> p j c u"
+                nc.scalar.copy(
+                    out=turned[t][:, half_of(h)].bitcast(F32).rearrange("p (j c u) -> p j c u", j=2, u=2),
+                    in_=banks[h][:].rearrange(runs, j=2, u=2),
+                )
+                give_back(("turned", t, h))
 
         def quantize_gradient(t):
             nc.vector.quantize_mx(out=g_codes[t][:].bitcast(FP8X4), scales=g_scales[t][:], in_=turned[t][:])
 
-        step = {}
-
-        def second_passes(dst, t, first, width):
+        def second_passes(acc, t, first, width):
             h, offset = divmod(first, HALF)
             for g in range(D_PASSES):
                 cols = slice(g * P, (g + 1) * P)
-                nc.tensor.matmul_mx(out=dst, lhsT=g_codes[t][:, cols].bitcast(FP8X4), lhsT_scale=g_scales[t][:, cols],
-                                    rhs=inv_words[h][g][:, 2 * offset : 2 * (offset + width)].bitcast(FP4X4),
-                                    rhs_scale=inv_scales[:, g, first : first + width], start=(g == 0), stop=(g == D_PASSES - 1))
+                nc.tensor.matmul_mx(
+                    out=acc,
+                    lhsT=g_codes[t][:, cols].bitcast(FP8X4),
+                    lhsT_scale=g_scales[t][:, cols],
+                    rhs=inv_words[h][g][:, FP4_BYTES * offset : FP4_BYTES * (offset + width)].bitcast(FP4X4),
+                    rhs_scale=inv_scales[h][:, g, offset : offset + width],
+                    start=(g == 0),
+                    stop=(g == D_PASSES - 1),
+                )
 
-        def second_group(t, f, b):
-            step[t, f] = bank(b)
-            second_passes(step[t, f][:], t, f * N, N)
+        def second_groups(t, chunks):
+            for f in chunks:
+                second_passes(take_bank(("step", t, f * CHUNK))[:], t, f * CHUNK, CHUNK)
 
-        def add_and_store(src, t, first, width):
+        def add_and_store(t, first, width):
             h, offset = divmod(first, HALF)
             result = stage.tile([P, width], F32, name="result", bufs=8, align_bytes=64)
-            nc.vector.tensor_tensor(out=result[:], in0=src, in1=x_sb[t][h][:, offset : offset + width], op=ALU.add)
+            nc.vector.tensor_tensor(
+                out=result[:], in0=held["step", t, first][1][:, 0:width], in1=x_sb[t][h][:, offset : offset + width], op=ALU.add
+            )
+            give_back(("step", t, first))
             nc.sync.dma_start(out=out[t * P : (t + 1) * P, first : first + width], in_=result[:])
 
-        def finish(t, f):
-            add_and_store(step[t, f][:], t, f * N, N)
+        def finish(t, chunks):
+            for f in chunks:
+                add_and_store(t, f * CHUNK, CHUNK)
 
-        whole = slice(0, N)
-        left, right = slice(0, N // 2), slice(N // 2, N)
-
-        clear(lo_scales[0])
-        clear(lo_scales[1])
-        clear(inv_scales)
+        for plane in lo_scales + inv_scales:
+            nc.vector.memset(plane[:].rearrange("p g n -> p (g n)").bitcast(I32), 0)
         make_identity(nc, ident[:])
 
         load_r(0)
         nc.sync.dma_start(out=lam_rows[:], in_=lam.rearrange("(p m) -> p m", p=P))
-        load_scales(lo_scales[0], a_lo_scales[:, :, 0:HALF])
-        load_lo(0, 0)
+        load_scales(lo_scales[0], a_lo_scales, 0)
+        load_words(lo_words[0][0], a_lo_words[0], 0)
         for s in range(1, LO_PASSES):
             load_r(s)
-            load_lo(0, s)
-        load_r(HI_PASS)
+            load_words(lo_words[0][s], a_lo_words[s], 0)
         load_hi(0)
+        load_r(HI_PASS)
         load_hi(1)
         load_x(0, 0)
-        load_scales(lo_scales[1], a_lo_scales[:, :, HALF:D])
-        load_lo(1, 0)
-        load_x(1, 0)
-        for s in range(1, LO_PASSES):
-            load_lo(1, s)
+        load_scales(lo_scales[1], a_lo_scales, 1)
+        for s in range(LO_PASSES):
+            load_words(lo_words[1][s], a_lo_words[s], 1)
+            if s == 1:
+                load_x(1, 0)
         load_hi(2)
         load_hi(3)
-        load_x(0, 1)
-        load_x(1, 1)
-        load_scales(inv_scales, hinv_scales)
-        load_x(2, 0)
-        for g in range(D_PASSES):
-            load_inv(0, g)
-        load_x(2, 1)
-        for g in range(D_PASSES):
-            load_inv(1, g)
+        for h, x_parts in enumerate((((0, 1), (1, 1)), ((2, 0), (2, 1)))):
+            for t, x_half in x_parts:
+                load_x(t, x_half)
+            load_scales(inv_scales[h], hinv_scales, h)
+            for g in range(D_PASSES):
+                load_words(inv_words[h][g], hinv_words[g], h)
         load_x(3, 0)
         load_x(3, 1)
 
+        grouped_r = interleave(r_raw[0])
+        quantize(grouped_r, r_codes[0], r_scales[0], left)
+        quantize(grouped_r, r_codes[0], r_scales[0], right)
 
-        def sweep(targets, features, s):
-            for t in targets:
-                for f in features:
-                    first_pass(t, f, s, s == 0, s == HI_PASS)
-
-        def shared(raw, codes, scales):
-            grouped = fresh_grouped()
-            interleave(True, grouped, raw, left)
-            interleave(False, grouped, raw, right)
-            quantize(grouped, codes, scales, whole)
-
-        def on_scalar(raw):
-            grouped = fresh_grouped()
-            interleave(False, grouped, raw, whole)
-            return grouped
-
-        g0 = fresh_grouped()
-        interleave(True, g0, r_raw[0], left)
-        interleave(False, g0, r_raw[0], right)
-        quantize(g0, r_codes[0], r_scales[0], left)
-        quantize(g0, r_codes[0], r_scales[0], right)
         lam_words = lam_rows[:].bitcast(F32)
-        for half in range(2):
-            spread = bank(6 + half)
+        lam_banks = [take_bank(("lam", part)) for part in range(2)]
+        for part in range(2):
             for j in range(4):
-                column = lam_words[:, 4 * half + j : 4 * half + j + 1]
-                nc.tensor.transpose(spread[:, j * P : (j + 1) * P], column.to_broadcast([P, P]), ident[:])
-            nc.scalar.copy(out=lam_all[:].bitcast(F32).rearrange("p (n j) -> p n j", j=8)[:, :, 4 * half : 4 * half + 4],
-                           in_=spread[:].rearrange("p (j n) -> p n j", j=4))
-        for t in range(4):
-            for f in range(2):
-                acc[t, f] = bank(2 * t + f)
-        sweep(range(4), range(2), 0)
-        for s in range(1, LO_PASSES):
-            shared(r_raw[s], r_codes[s], r_scales[s])
-            sweep(range(4), range(2), s)
-        shared(r_raw[HI_PASS], r_codes[HI_PASS], r_scales[HI_PASS])
-        for f in range(2):
-            shared(hi_raw[f], hi_codes[f], hi_scales[f])
-            sweep((2, 3, 0, 1) if f == 0 else (0, 2, 3, 1), [f], HI_PASS)
+                column = lam_words[:, 4 * part + j : 4 * part + j + 1]
+                nc.tensor.transpose(lam_banks[part][:, j * P : (j + 1) * P], column.to_broadcast([P, P]), ident[:])
+            nc.scalar.copy(
+                out=lam_all[:].bitcast(F32).rearrange("p (n j) -> p n j", j=8)[:, :, 4 * part : 4 * part + 4],
+                in_=lam_banks[part][:].rearrange("p (j n) -> p n j", j=4),
+            )
+            give_back(("lam", part))
 
-        V = nc.vector
-        R = nc.gpsimd
-        park(2, 0)
-        park(3, 0)
-        ridge_term(0, 0, V)
-        park(2, 1)
-        park(3, 1)
+        first_passes(range(TILES), (0, 1), [0])
+        for s in range(1, LO_PASSES):
+            quantize(interleave(r_raw[s]), r_codes[s], r_scales[s])
+            first_passes(range(TILES), (0, 1), [s])
+        grouped_hi0 = interleave(hi_raw[0])
+        grouped_r = interleave(r_raw[HI_PASS], on_vector=right, on_scalar=left)
+        quantize(grouped_hi0, hi_codes[0], hi_scales[0])
+        quantize(grouped_r, r_codes[HI_PASS], r_scales[HI_PASS], right)
+        grouped_hi1 = interleave(hi_raw[1])
+        quantize(grouped_r, r_codes[HI_PASS], r_scales[HI_PASS], left)
+        quantize(grouped_hi1, hi_codes[1], hi_scales[1])
+        first_passes((2, 3, 0, 1), [0], [HI_PASS])
+        first_passes((0, 2, 3, 1), [1], [HI_PASS])
+        for f in range(2):
+            park(2, f)
+            park(3, f)
         park(1, 0)
         park(1, 1)
-        ridge_term(1, 0, V)
-        gradient(0, 0)
-        gradient(0, 1)
-        parked_gradient(1, 0)
-        for t, banks in enumerate(((4, 6), (5, 7), (2, 3))):
-            for f in range(2, 4):
-                acc[t, f] = bank(banks[f - 2])
-            for s in range(LO_PASSES):
-                sweep([t], range(2, 4), s)
-        shared(hi_raw[2], hi_codes[2], hi_scales[2])
-        g3 = fresh_grouped()
-        interleave(True, g3, hi_raw[3], left)
-        interleave(False, g3, hi_raw[3], right)
-        ridge_term(0, 1, V)
-        quantize(g3, hi_codes[3], hi_scales[3], whole)
-        for f in range(2, 4):
-            sweep(range(3), [f], HI_PASS)
-        ridge_term(1, 1, V)
-        ridge_term(2, 0, R)
-        gradient(0, 2)
-        gradient(0, 3)
-        acc[3, 2] = bank(0)
-        for s in range(2):
-            first_pass(3, 2, s, s == 0, False)
-        turn(0, (1, 4))
-        for s in range(2, LO_PASSES + 1):
-            first_pass(3, 2, s, False, s == HI_PASS)
-        gradient(1, 2)
-        gradient(1, 3)
-        ridge_term(2, 1, R)
-        first_group(3, 3, 6)
+        ridge_term(0, 0)
+        gradient_from_bank(0, 0)
+        gradient_from_bank(0, 1)
+        ridge_term(1, 0)
+        gradient_from_parked(1, 0)
+
+        first_passes((0, 1), (2, 3), range(LO_PASSES))
+        first_passes([2], (2, 3), range(LO_PASSES))
+        first_passes([3], [2], range(LO_PASSES))
+        grouped_hi2 = interleave(hi_raw[2])
+        grouped_hi3 = interleave(hi_raw[3])
+        quantize(grouped_hi2, hi_codes[2], hi_scales[2])
+        quantize(grouped_hi3, hi_codes[3], hi_scales[3])
+        ridge_term(0, 1)
+        ridge_term(1, 1)
+        first_passes(range(TILES), [2], [HI_PASS])
+        first_passes(range(TILES - 1), [3], [HI_PASS])
+        park(2, 2)
+        park(3, 2)
+        park(2, 3)
+        gradient_from_bank(0, 2)
+        gradient_from_bank(0, 3)
+        first_passes([3], [3], range(AHEAD_OF_TURN))
+        turn(0)
+        first_passes([3], [3], range(AHEAD_OF_TURN, LO_PASSES + 1))
+        gradient_from_bank(1, 2)
+        gradient_from_bank(1, 3)
         quantize_gradient(0)
-        second_group(0, 0, 5)
-        turn(1, (7, 1))
-        parked_gradient(2, 0)
-        gradient(2, 2)
-        gradient(2, 3)
-        ridge_term(3, 0, R)
-        ridge_term(3, 1, R)
-        second_group(0, 1, 4)
+        turn(1)
+        park(3, 3)
+
+        ridge_term(2, 0)
+        second_groups(0, (0, 1))
         quantize_gradient(1)
-        finish(0, 0)
-        second_group(0, 2, 2)
-        second_group(0, 3, 3)
-        finish(0, 1)
-        turn(2, (7, 1))
-        finish(0, 2)
-        finish(0, 3)
-        second_group(1, 0, 5)
-        second_group(1, 1, 4)
-        finish(1, 0)
+        ridge_term(2, 1)
+        gradient_from_parked(2, 0)
+        gradient_from_parked(2, 1)
+        second_groups(1, (0, 1))
+        finish(0, (0, 1))
+        turn(2)
+        ridge_term(3, 0)
+        second_groups(0, (2, 3))
+        finish(1, (0, 1))
         quantize_gradient(2)
-        parked_gradient(3, 0)
-        gradient(3, 2)
-        gradient(3, 3)
-        second_group(1, 2, 2)
-        second_group(1, 3, 3)
-        finish(1, 1)
-        second_group(2, 0, 5)
-        second_group(2, 1, 0)
-        turn(3, (7, 1))
-        finish(1, 2)
-        finish(1, 3)
-        second_group(2, 2, 6)
-        finish(2, 0)
+        ridge_term(3, 1)
+        second_groups(1, (2, 3))
+        gradient_from_parked(3, 0)
+        gradient_from_parked(3, 1)
+        second_groups(2, (0, 1))
+        finish(0, (2, 3))
+        turn(3)
+        finish(1, (2, 3))
+        second_groups(2, (2, 3))
         quantize_gradient(3)
-        second_group(2, 3, 4)
-        finish(2, 1)
-        finish(2, 2)
-        second_group(3, 0, 2)
-        second_group(3, 1, 3)
-        second_group(3, 2, 5)
-        finish(2, 3)
-        finish(3, 0)
-        finish(3, 1)
-        pieces = []
-        for b, first, width in ((0, 3 * N, 2 * P), (7, 3 * N + 2 * P, P), (1, 3 * N + 3 * P, P)):
-            piece = bank(b)
-            for q in range(0, width, P):
-                second_passes(piece[:, q : q + P], 3, first + q, P)
-            pieces.append((piece[:, 0:width], 3, first, width))
-        finish(3, 2)
-        for piece in pieces:
-            add_and_store(*piece)
+        finish(2, (0, 1))
+        second_groups(3, (0, 1, 2))
+        finish(2, (2, 3))
+        finish(3, (0, 1))
+        pieces = ((3 * CHUNK, 2 * P), (3 * CHUNK + 2 * P, P), (3 * CHUNK + 3 * P, P))
+        for first, width in pieces:
+            acc = take_bank(("step", 3, first))
+            for offset in range(0, width, P):
+                second_passes(acc[:, offset : offset + P], 3, first + offset, P)
+        finish(3, [2])
+        for first, width in pieces:
+            add_and_store(3, first, width)

from contextlib import ExitStack

import concourse.mybir as mybir
from concourse.masks import make_identity

C, D, HI, LO = 512, 2048, 512, 2048
FLOPS = 2 * C * D * (HI + LO) + 2 * C * D * D

F32 = mybir.dt.float32
BF16 = mybir.dt.bfloat16
I32 = mybir.dt.int32
U32 = mybir.dt.uint32
U8 = mybir.dt.uint8
FP8X4 = mybir.dt.float8_e4m3fn_x4
FP4X4 = mybir.dt.float4_e2m1fn_x4
ALU = mybir.AluOpType

P = 128
PACK = 4
K_PASS = P * PACK
CHUNK = 512
HALF = 2 * CHUNK
TILES = C // P
CHUNKS = D // CHUNK
LO_PASSES = LO // K_PASS
HI_PASS = LO_PASSES
D_PASSES = D // K_PASS
BANKS = 8
FP4_BYTES = 2
AHEAD_OF_TURN = 2


def tile_hessian_sketch_step_s3_kernel(
    tc, x, r_hi, a_hi, r_lo, a_lo_words, a_lo_scales, lam, hinv_words, hinv_scales, out
):
    nc = tc.nc
    with ExitStack() as ctx:
        keep = ctx.enter_context(tc.tile_pool(name="keep", bufs=1))
        stage = ctx.enter_context(tc.tile_pool(name="stage", bufs=4))
        psum = ctx.enter_context(tc.psum_pool(name="psum", bufs=1))
        ctx.enter_context(tc.manual_schedule())

        def kept(name, shape, dtype):
            return keep.tile(shape, dtype, name=name, align_bytes=64)

        ident = kept("ident", [P, P], F32)
        lam_rows = kept("lam_rows", [P, D // P], BF16)
        lam_all = kept("lam_all", [P, D], BF16)
        r_raw = [kept("r_raw%d" % s, [P, PACK, C], BF16) for s in range(LO_PASSES + 1)]
        r_codes = [kept("r_codes%d" % s, [P, C], U32) for s in range(LO_PASSES + 1)]
        r_scales = [kept("r_scales%d" % s, [P, C], U8) for s in range(LO_PASSES + 1)]
        hi_raw = [kept("hi_raw%d" % f, [P, PACK, CHUNK], BF16) for f in range(CHUNKS)]
        hi_codes = [kept("hi_codes%d" % f, [P, CHUNK], U32) for f in range(CHUNKS)]
        hi_scales = [kept("hi_scales%d" % f, [P, CHUNK], U8) for f in range(CHUNKS)]
        lo_words = [[kept("lo_words%d_%d" % (h, s), [P, FP4_BYTES * HALF], U8) for s in range(LO_PASSES)] for h in range(2)]
        lo_scales = [kept("lo_scales%d" % h, [P, LO_PASSES, HALF], U8) for h in range(2)]
        inv_words = [[kept("inv_words%d_%d" % (h, g), [P, FP4_BYTES * HALF], U8) for g in range(D_PASSES)] for h in range(2)]
        inv_scales = [kept("inv_scales%d" % h, [P, D_PASSES, HALF], U8) for h in range(2)]
        x_sb = [[kept("x%d_%d" % (t, h), [P, HALF], BF16) for h in range(2)] for t in range(TILES)]
        grad = [[kept("grad%d_%d" % (t, h), [P, HALF], BF16) for h in range(2)] for t in range(TILES)]
        g_codes = [kept("g_codes%d" % t, [P, D_PASSES * P], U32) for t in range(TILES)]
        g_scales = [kept("g_scales%d" % t, [P, D_PASSES * P], U8) for t in range(TILES)]

        free_banks = list(range(BANKS))
        held = {}

        def take_bank(key):
            b = free_banks[0]
            free_banks.remove(b)
            held[key] = (b, psum.tile([P, CHUNK], F32, name="bank%d" % b))
            return held[key][1]

        def give_back(key):
            free_banks.append(held[key][0])

        def half_of(h, bytes_a_column=1):
            return slice(h * HALF * bytes_a_column, (h + 1) * HALF * bytes_a_column)

        def load_rows(dst, rows):
            nc.sync.dma_start(out=dst[:], in_=rows.rearrange("(p t) w -> p t w", t=PACK))

        def load_r(s):
            load_rows(r_raw[s], r_hi if s == HI_PASS else r_lo[s * K_PASS : (s + 1) * K_PASS, :])

        def load_hi(f):
            load_rows(hi_raw[f], a_hi[:, f * CHUNK : (f + 1) * CHUNK])

        def load_words(dst, words, h):
            nc.sync.dma_start(out=dst[:].bitcast(I32), in_=words[:, half_of(h, FP4_BYTES)].bitcast(I32))

        def load_scales(dst, scales, h):
            rows = scales[:, :, half_of(h)].rearrange("g (q r) n -> r q g n", r=4)
            for r in range(4):
                nc.sync.dma_start(out=dst[r:P:32, :, :].bitcast(I32), in_=rows[r].bitcast(I32))

        def load_x(t, h):
            nc.sync.dma_start(out=x_sb[t][h][:], in_=x[t * P : (t + 1) * P, half_of(h)])

        whole = slice(0, CHUNK)
        left, right = slice(0, CHUNK // 2), slice(CHUNK // 2, CHUNK)

        def interleave(raw, on_vector=left, on_scalar=right):
            grouped = stage.tile([P, CHUNK, PACK], BF16, name="grouped", align_bytes=64)
            dst, src = "p (c i) t -> p c t i", "p t (c i) -> p c t i"
            nc.vector.tensor_copy(out=grouped[:, on_vector, :].rearrange(dst, i=4), in_=raw[:, :, on_vector].rearrange(src, i=4))
            nc.scalar.copy(out=grouped[:, on_scalar, :].rearrange(dst, i=4), in_=raw[:, :, on_scalar].rearrange(src, i=4))
            return grouped

        def quantize(grouped, codes, scales, cols=whole):
            nc.vector.quantize_mx(
                out=codes[:, cols].bitcast(FP8X4),
                scales=scales[:, cols],
                in_=grouped[:, cols, :].rearrange("p c t -> p (c t)"),
            )

        def first_pass(t, f, s):
            acc = take_bank(("sums", t, f)) if s == 0 else held["sums", t, f][1]
            cols = slice(t * P, (t + 1) * P)
            if s == HI_PASS:
                rhs, rhs_scale = hi_codes[f][:].bitcast(FP8X4), hi_scales[f][:]
            else:
                h, j = divmod(f, 2)
                rhs = lo_words[h][s][:, j * FP4_BYTES * CHUNK : (j + 1) * FP4_BYTES * CHUNK].bitcast(FP4X4)
                rhs_scale = lo_scales[h][:, s, j * CHUNK : (j + 1) * CHUNK]
            nc.tensor.matmul_mx(
                out=acc[:],
                lhsT=r_codes[s][:, cols].bitcast(FP8X4),
                lhsT_scale=r_scales[s][:, cols],
                rhs=rhs,
                rhs_scale=rhs_scale,
                start=(s == 0),
                stop=(s == HI_PASS),
            )

        def first_passes(tiles, chunks, passes):
            for s in passes:
                for t in tiles:
                    for f in chunks:
                        first_pass(t, f, s)

        ridge, parked, turned = {}, {}, {}

        def ridge_term(t, h):
            ridge[t, h] = stage.tile([P, HALF], F32, name="ridge", bufs=3, align_bytes=64)
            nc.vector.tensor_tensor(out=ridge[t, h][:], in0=x_sb[t][h][:], in1=lam_all[:, half_of(h)], op=ALU.mult)

        def park(t, f):
            h, j = divmod(f, 2)
            if (t, h) not in parked:
                parked[t, h] = stage.tile([P, HALF], F32, name="parked", bufs=5, align_bytes=64)
            nc.scalar.copy(out=parked[t, h][:, j * CHUNK : (j + 1) * CHUNK], in_=held["sums", t, f][1][:])
            give_back(("sums", t, f))

        def gradient_from_bank(t, f):
            h, j = divmod(f, 2)
            cols = slice(j * CHUNK, (j + 1) * CHUNK)
            nc.vector.tensor_tensor(
                out=grad[t][h][:, cols].rearrange("c (u p e) -> c u p e", u=2, e=2),
                in0=held["sums", t, f][1][:].rearrange("c (p u e) -> c u p e", u=2, e=2),
                in1=ridge[t, h][:, cols].rearrange("c (p u e) -> c u p e", u=2, e=2),
                op=ALU.subtract,
            )
            give_back(("sums", t, f))

        def gradient_from_parked(t, h):
            nc.vector.tensor_tensor(
                out=grad[t][h][:].rearrange("c (u q e) -> c u q e", u=2, e=2),
                in0=parked[t, h][:].rearrange("c (q u e) -> c u q e", u=2, e=2),
                in1=ridge[t, h][:].rearrange("c (q u e) -> c u q e", u=2, e=2),
                op=ALU.subtract,
            )

        def turn(t):
            turned[t] = stage.tile([P, D], BF16, name="turned", bufs=2, align_bytes=64)
            banks = [take_bank(("turned", t, h)) for h in range(2)]
            for h in range(2):
                words = grad[t][h][:].bitcast(F32)
                for run in range(4):
                    nc.tensor.transpose(banks[h][:, run * P : (run + 1) * P], words[:, run * P : (run + 1) * P], ident[:])
                runs = "p (u j c) -> p j c u" if (t, h) in parked else "p (j u c) -> p j c u"
                nc.scalar.copy(
                    out=turned[t][:, half_of(h)].bitcast(F32).rearrange("p (j c u) -> p j c u", j=2, u=2),
                    in_=banks[h][:].rearrange(runs, j=2, u=2),
                )
                give_back(("turned", t, h))

        def quantize_gradient(t):
            nc.vector.quantize_mx(out=g_codes[t][:].bitcast(FP8X4), scales=g_scales[t][:], in_=turned[t][:])

        def second_passes(acc, t, first, width):
            h, offset = divmod(first, HALF)
            for g in range(D_PASSES):
                cols = slice(g * P, (g + 1) * P)
                nc.tensor.matmul_mx(
                    out=acc,
                    lhsT=g_codes[t][:, cols].bitcast(FP8X4),
                    lhsT_scale=g_scales[t][:, cols],
                    rhs=inv_words[h][g][:, FP4_BYTES * offset : FP4_BYTES * (offset + width)].bitcast(FP4X4),
                    rhs_scale=inv_scales[h][:, g, offset : offset + width],
                    start=(g == 0),
                    stop=(g == D_PASSES - 1),
                )

        def second_groups(t, chunks):
            for f in chunks:
                second_passes(take_bank(("step", t, f * CHUNK))[:], t, f * CHUNK, CHUNK)

        def add_and_store(t, first, width):
            h, offset = divmod(first, HALF)
            result = stage.tile([P, width], F32, name="result", bufs=8, align_bytes=64)
            nc.vector.tensor_tensor(
                out=result[:], in0=held["step", t, first][1][:, 0:width], in1=x_sb[t][h][:, offset : offset + width], op=ALU.add
            )
            give_back(("step", t, first))
            nc.sync.dma_start(out=out[t * P : (t + 1) * P, first : first + width], in_=result[:])

        def finish(t, chunks):
            for f in chunks:
                add_and_store(t, f * CHUNK, CHUNK)

        for plane in lo_scales + inv_scales:
            nc.vector.memset(plane[:].rearrange("p g n -> p (g n)").bitcast(I32), 0)
        make_identity(nc, ident[:])

        load_r(0)
        nc.sync.dma_start(out=lam_rows[:], in_=lam.rearrange("(p m) -> p m", p=P))
        load_scales(lo_scales[0], a_lo_scales, 0)
        load_words(lo_words[0][0], a_lo_words[0], 0)
        for s in range(1, LO_PASSES):
            load_r(s)
            load_words(lo_words[0][s], a_lo_words[s], 0)
        load_hi(0)
        load_r(HI_PASS)
        load_hi(1)
        load_x(0, 0)
        load_scales(lo_scales[1], a_lo_scales, 1)
        for s in range(LO_PASSES):
            load_words(lo_words[1][s], a_lo_words[s], 1)
            if s == 1:
                load_x(1, 0)
        load_hi(2)
        load_hi(3)
        for h, x_parts in enumerate((((0, 1), (1, 1)), ((2, 0), (2, 1)))):
            for t, x_half in x_parts:
                load_x(t, x_half)
            load_scales(inv_scales[h], hinv_scales, h)
            for g in range(D_PASSES):
                load_words(inv_words[h][g], hinv_words[g], h)
        load_x(3, 0)
        load_x(3, 1)

        grouped_r = interleave(r_raw[0])
        quantize(grouped_r, r_codes[0], r_scales[0], left)
        quantize(grouped_r, r_codes[0], r_scales[0], right)

        lam_words = lam_rows[:].bitcast(F32)
        lam_banks = [take_bank(("lam", part)) for part in range(2)]
        for part in range(2):
            for j in range(4):
                column = lam_words[:, 4 * part + j : 4 * part + j + 1]
                nc.tensor.transpose(lam_banks[part][:, j * P : (j + 1) * P], column.to_broadcast([P, P]), ident[:])
            nc.scalar.copy(
                out=lam_all[:].bitcast(F32).rearrange("p (n j) -> p n j", j=8)[:, :, 4 * part : 4 * part + 4],
                in_=lam_banks[part][:].rearrange("p (j n) -> p n j", j=4),
            )
            give_back(("lam", part))

        first_passes(range(TILES), (0, 1), [0])
        for s in range(1, LO_PASSES):
            quantize(interleave(r_raw[s]), r_codes[s], r_scales[s])
            first_passes(range(TILES), (0, 1), [s])
        grouped_hi0 = interleave(hi_raw[0])
        grouped_r = interleave(r_raw[HI_PASS], on_vector=right, on_scalar=left)
        quantize(grouped_hi0, hi_codes[0], hi_scales[0])
        quantize(grouped_r, r_codes[HI_PASS], r_scales[HI_PASS], right)
        grouped_hi1 = interleave(hi_raw[1])
        quantize(grouped_r, r_codes[HI_PASS], r_scales[HI_PASS], left)
        quantize(grouped_hi1, hi_codes[1], hi_scales[1])
        first_passes((2, 3, 0, 1), [0], [HI_PASS])
        first_passes((0, 2, 3, 1), [1], [HI_PASS])
        for f in range(2):
            park(2, f)
            park(3, f)
        park(1, 0)
        park(1, 1)
        ridge_term(0, 0)
        gradient_from_bank(0, 0)
        gradient_from_bank(0, 1)
        ridge_term(1, 0)
        gradient_from_parked(1, 0)

        first_passes((0, 1), (2, 3), range(LO_PASSES))
        first_passes([2], (2, 3), range(LO_PASSES))
        first_passes([3], [2], range(LO_PASSES))
        grouped_hi2 = interleave(hi_raw[2])
        grouped_hi3 = interleave(hi_raw[3])
        quantize(grouped_hi2, hi_codes[2], hi_scales[2])
        quantize(grouped_hi3, hi_codes[3], hi_scales[3])
        ridge_term(0, 1)
        ridge_term(1, 1)
        first_passes(range(TILES), [2], [HI_PASS])
        first_passes(range(TILES - 1), [3], [HI_PASS])
        park(2, 2)
        park(3, 2)
        park(2, 3)
        gradient_from_bank(0, 2)
        gradient_from_bank(0, 3)
        first_passes([3], [3], range(AHEAD_OF_TURN))
        turn(0)
        first_passes([3], [3], range(AHEAD_OF_TURN, LO_PASSES + 1))
        gradient_from_bank(1, 2)
        gradient_from_bank(1, 3)
        quantize_gradient(0)
        turn(1)
        park(3, 3)

        ridge_term(2, 0)
        second_groups(0, (0, 1))
        quantize_gradient(1)
        ridge_term(2, 1)
        gradient_from_parked(2, 0)
        gradient_from_parked(2, 1)
        second_groups(1, (0, 1))
        finish(0, (0, 1))
        turn(2)
        ridge_term(3, 0)
        second_groups(0, (2, 3))
        finish(1, (0, 1))
        quantize_gradient(2)
        ridge_term(3, 1)
        second_groups(1, (2, 3))
        gradient_from_parked(3, 0)
        gradient_from_parked(3, 1)
        second_groups(2, (0, 1))
        finish(0, (2, 3))
        turn(3)
        finish(1, (2, 3))
        second_groups(2, (2, 3))
        quantize_gradient(3)
        finish(2, (0, 1))
        second_groups(3, (0, 1, 2))
        finish(2, (2, 3))
        finish(3, (0, 1))
        pieces = ((3 * CHUNK, 2 * P), (3 * CHUNK + 2 * P, P), (3 * CHUNK + 3 * P, P))
        for first, width in pieces:
            acc = take_bank(("step", 3, first))
            for offset in range(0, width, P):
                second_passes(acc[:, offset : offset + P], 3, first + offset, P)
        finish(3, [2])
        for first, width in pieces:
            add_and_store(3, first, width)
